import numpy as np
import ml_dtypes


def mxq(x, axis, fmt="e4m3"):
    dtype, down = {"e4m3": (ml_dtypes.float8_e4m3fn, 7), "e5m2": (ml_dtypes.float8_e5m2, 14)}[fmt]
    v = np.moveaxis(np.asarray(x, np.float32).astype(ml_dtypes.bfloat16).astype(np.float64), axis, -1)
    blocks = v.reshape(v.shape[:-1] + (-1, 32))
    amax = np.abs(blocks).max(-1, keepdims=True)
    byte = np.maximum(np.where(amax > 0, np.frexp(amax)[1] - 1 + 127, 0) - down, 1)
    scale = np.exp2(byte - 127.0)
    codes = (blocks / scale).astype(np.float32).astype(dtype).astype(np.float64)
    return np.moveaxis((codes * scale).reshape(v.shape), -1, axis)


WIDE = False


def mx_kscale(k):
    if not WIDE:
        return np.ones(k)
    levels = np.array([10, -10, 5, -5, 0])
    if k % 512:
        return np.exp2(np.random.permutation(np.resize(levels, k // 32))).repeat(32)
    a = np.empty((k // 512, 16))
    for p in range(k // 512):
        a[p, :8] = np.random.permutation(np.resize(levels, 8))
        for g in range(8):
            far = levels[np.abs(levels - a[p, g]) >= 10]
            a[p, g + 8] = far[np.random.randint(len(far))]
    return np.exp2(a.ravel()).repeat(32)


def f64(x):
    return np.asarray(x).astype(np.float64)


def striped(idx):
    return np.tile(idx.reshape(-1, 16).T, (8, 1)).astype(np.uint16)


def unstriped(offs):
    return offs[:16].T.reshape(-1).astype(np.int64)


def striped8(idx):
    return np.concatenate([x.reshape(-1, 16).T for x in idx]).astype(np.uint16)


def runs(offs, k):
    lists = np.stack([offs[16 * r : 16 * r + 16].T.reshape(-1) for r in range(8)]).astype(np.int64)
    return lists[np.arange(k) % 512 // 64]


def pack_weight(w):
    k, n = w.shape
    w = f64(np.asarray(w, np.float32).astype(ml_dtypes.bfloat16)).reshape(k // 32, 32, n)
    amax = np.abs(w).max(1)
    byte = np.clip(np.where(amax > 0, np.frexp(amax)[1] - 1 + 127 - 7, 1), 1, 254)
    scaled = (w * np.exp2(127.0 - byte)[:, None, :]).reshape(k, n).astype(np.float32)
    words = np.ascontiguousarray(scaled.reshape(k // 512, 128, 4, n).transpose(0, 1, 3, 2)).astype(ml_dtypes.float8_e4m3fn).view(np.uint8)
    return words, np.ascontiguousarray(byte.astype(np.uint8).reshape(k // 512, 16, n))


def unpack_weight(words, scales):
    g, p, n, _ = words.shape
    vals = np.ascontiguousarray(words).view(ml_dtypes.float8_e4m3fn).astype(np.float64) * np.repeat(np.exp2(scales.astype(np.float64) - 127.0), 8, axis=1)[..., None]
    return vals.transpose(0, 1, 3, 2).reshape(g * 512, n)


def sigmoid(v):
    return 1.0 / (1.0 + np.exp(-np.maximum(v, -700.0)))

def planes(y):
    n, m = y.shape
    v = y.astype(np.float32).astype(ml_dtypes.bfloat16).astype(np.float64).reshape(n // 32, 32, m)
    top = np.abs(v).max(1)
    byte = np.clip(np.where(top > 0, np.frexp(top)[1] - 1 + 127 - 7, 1), 1, 254)
    codes = (v * np.exp2(127.0 - byte)[:, None, :]).reshape(n, m).astype(np.float32).astype(ml_dtypes.float8_e4m3fn).view(np.uint8)
    words = codes.reshape(n // 512, 128, 4, m).transpose(0, 1, 3, 2)
    return np.ascontiguousarray(words), np.ascontiguousarray(byte.astype(np.uint8).reshape(n // 512, 16, m))


K, T, S, G, H, W = 512, 2048, 512, 2048, 512, 256


def setup_inputs():
    n = np.random.standard_normal
    s = mx_kscale(K)[:, None]
    packed_xT = pack_weight(n((K, T)) * s)
    packed_dT = pack_weight(n((K, G)) / s)
    perm = np.stack([np.random.permutation(S) for _ in range(8)])
    return {
        "x_words": packed_xT[0],
        "x_scales": packed_xT[1],
        "d_words": packed_dT[0],
        "d_scales": packed_dT[1],
        "gs": (np.random.uniform(0.5, 1.5, (K, 1)) * s).astype(np.float32),
        "offs": striped(np.random.permutation(T)[:S]),
        "k1": striped8(np.random.randint(0, G, (8, H))),
        "n1": striped8(perm[:, :W]),
        "n2": striped8(perm[:, W:]),
        "n3": striped8(np.stack([np.random.permutation(S) for _ in range(8)])),
        "n4": striped8(np.stack([np.random.permutation(S) for _ in range(8)])),
        "n5": striped8(np.stack([np.random.permutation(S) for _ in range(8)])),
    }


def reference(x_words, x_scales, d_words, d_scales, gs, offs, k1, n1, n2, n3, n4, n5):
    d_k1 = unpack_weight(d_words, d_scales)[np.arange(K)[:, None], runs(k1, K)]
    xq = unpack_weight(x_words, x_scales)[:, unstriped(offs)]
    h = 0.0625 * (d_k1.T @ xq)
    pa = h[np.arange(H)[:, None], runs(n1, H)]
    pb = h[np.arange(H)[:, None], runs(n2, H)]
    ra = pa - (0.5 * pb)
    ds = h.copy()
    ds[np.arange(H)[:, None], runs(n2, H)] = ra
    z = f64(gs) * (ds - (0.5 * (ds[np.arange(H)[:, None], runs(n3, H)])))
    h2 = 0.0625 * ((d_k1.T @ mxq(z, 0, "e4m3")))
    st = h2 * (sigmoid(h2[np.arange(H)[:, None], runs(n4, H)]))
    out_0 = st - (st[np.arange(H)[:, None], runs(n5, H)])
    return (out_0,) + planes(out_0)

@@ -1,0 +1,225 @@
+from contextlib import ExitStack
+
+import concourse.mybir as mybir
+
+F32 = mybir.dt.float32
+BF16 = mybir.dt.bfloat16
+I32 = mybir.dt.int32
+U32 = mybir.dt.uint32
+U16 = mybir.dt.uint16
+U8 = mybir.dt.uint8
+FP8X4 = mybir.dt.float8_e4m3fn_x4
+ALU = mybir.AluOpType
+ACT = mybir.ActivationFunctionType
+
+P = 128
+PACK = 4
+TABLE = 2048
+S = 512
+HALF = 256
+FLOPS = 2 * 2 * 512 * 512 * 512
+
+
+def tile_picked_ringfolddhopg_none_po_kernel(
+    tc, x_words, x_scales, d_words, d_scales, gs, offs, k1, n1, n2, n3, n4, n5, out_0, out_1, out_2
+):
+    nc = tc.nc
+    with ExitStack() as ctx:
+        keep = ctx.enter_context(tc.tile_pool(name="keep", bufs=1))
+        psum = ctx.enter_context(tc.psum_pool(name="psum", bufs=1))
+
+        def load_list(src, name):
+            t = keep.tile(list(src.shape), U16, name=name)
+            nc.sync.dma_start(t[:], src)
+            return t
+
+        def cols(hf):
+            return slice(hf * HALF, (hf + 1) * HALF)
+
+        def entries(lst, hf):
+            return lst[:, hf * (HALF // 16) : (hf + 1) * (HALF // 16)]
+
+        d_sc = keep.tile([P, TABLE], U8, name="d_sc")
+        x_sc = keep.tile([P, TABLE], U8, name="x_sc")
+        planes = keep.tile([P, 2 * S], U8, name="planes", align_bytes=64)
+        nc.vector.memset(planes[:].bitcast(I32), 0)
+
+        def load_scales(dst, src):
+            rows = src[0].bitcast(I32)
+            nc.sync.dma_start(dst[:].bitcast(I32), rows.unsqueeze(1).to_broadcast([16, 8, TABLE // 4]))
+
+        l_k1 = load_list(k1, "l_k1")
+        load_scales(d_sc, d_scales)
+        l_offs = load_list(offs, "l_offs")
+        load_scales(x_sc, x_scales)
+        l_n1 = load_list(n1, "l_n1")
+        l_n2 = load_list(n2, "l_n2")
+        d_w = keep.tile([P, TABLE], U32, name="d_w")
+        x_w = keep.tile([P, TABLE], U32, name="x_w")
+        nc.sync.dma_start(d_w[:].bitcast(I32), d_words[0].rearrange("p n t -> p (n t)").bitcast(I32))
+        nc.sync.dma_start(x_w[:].bitcast(I32), x_words[0].rearrange("p n t -> p (n t)").bitcast(I32))
+
+        d_bg = keep.tile([P, S], U8, name="d_bg")
+        x_bg = keep.tile([P, S], U8, name="x_bg")
+        staged = keep.tile([P, 2 * S], U8, name="staged")
+        nc.vector.tensor_copy(d_bg[:], d_sc[:].indirect(l_k1[:]))
+        nc.vector.tensor_copy(x_bg[:], x_sc[:].indirect(l_offs[:]))
+        nc.vector.tensor_copy(
+            staged[:, 0:S].rearrange("p (t m) -> p m t", t=PACK), d_bg[:].rearrange("p (m t) -> p m t", t=PACK)
+        )
+        nc.vector.tensor_copy(staged[:, S : 2 * S].bitcast(I32), x_bg[:].bitcast(I32))
+        for r in range(4):
+            nc.scalar.dma_start(planes[r:P:32, :].bitcast(I32), staged[8 * r : P : 32, :].bitcast(I32))
+
+        l_n3 = load_list(n3, "l_n3")
+        g_s = keep.tile([P, PACK], F32, name="g_s")
+        nc.gpsimd.dma_start(g_s[:], gs.rearrange("(p t) o -> p (t o)", t=PACK))
+        l_n4 = load_list(n4, "l_n4")
+        l_n5 = load_list(n5, "l_n5")
+
+        d_wg = keep.tile([P, S], U32, name="d_wg")
+        d_wd = keep.tile([P, S], U32, name="d_wd", align_bytes=64)
+        nc.vector.tensor_copy(d_wg[:], d_w[:].indirect(l_k1[:]))
+        nc.vector.tensor_copy(
+            d_wd[:].rearrange("p (t m) -> p m t", t=PACK), d_wg[:].rearrange("p (m t) -> p m t", t=PACK)
+        )
+        x_wg = [keep.tile([P, HALF], U32, name="x_wg%d" % hf, align_bytes=64) for hf in range(2)]
+
+        def product(t, hf, codes, scales):
+            acc = psum.tile([P, HALF], F32, name="acc%d%d" % (t, hf), tag="acc%d%d" % (t, hf))
+            nc.tensor.matmul_mx(
+                out=acc[:],
+                lhsT=d_wd[:, t * P : (t + 1) * P].bitcast(FP8X4),
+                lhsT_scale=planes[:, t * P : (t + 1) * P],
+                rhs=codes.bitcast(FP8X4),
+                rhs_scale=scales,
+                start=True,
+                stop=True,
+            )
+            return acc
+
+        def evac(on_vector, dst, acc):
+            if on_vector:
+                nc.vector.tensor_scalar(dst, acc[:], 0.0625, None, ALU.mult)
+            else:
+                nc.scalar.activation(dst, acc[:], ACT.Copy, scale=0.0625)
+
+        def fetch(on_vector, dst, window, lst):
+            if on_vector:
+                nc.vector.tensor_copy(dst, window[:].indirect(lst))
+            else:
+                nc.scalar.activation(dst, window[:].indirect(lst), ACT.Copy)
+
+        acc1 = {}
+        for hf in range(2):
+            nc.vector.tensor_copy(x_wg[hf][:], x_w[:].indirect(entries(l_offs, hf)))
+        for t, hf in ((0, 0), (1, 0), (0, 1), (1, 1), (2, 0), (2, 1), (3, 0), (3, 1)):
+            acc1[t, hf] = product(t, hf, x_wg[hf][:], planes[:, S + hf * HALF : S + (hf + 1) * HALF])
+
+        ds = [keep.tile([P, S], F32, name="ds%d" % t) for t in range(PACK)]
+
+        def pair_up(t):
+            pa = keep.tile([P, HALF], F32, name="pa%d" % t)
+            pb = keep.tile([P, HALF], F32, name="pb%d" % t)
+            nc.scalar.activation(pb[:], ds[t][:].indirect(l_n2[:]), ACT.Copy, scale=-0.5)
+            fetch(t == 0, pa[:], ds[t], l_n1[:])
+            nc.vector.tensor_tensor(ds[t][:].indirect(l_n2[:]), pa[:], pb[:], ALU.add)
+
+        for t in range(2):
+            evac(False, ds[t][:, cols(0)], acc1[t, 0])
+            evac(True, ds[t][:, cols(1)], acc1[t, 1])
+        pair_up(0)
+        pair_up(1)
+        for t in range(2, PACK):
+            evac(False, ds[t][:, cols(0)], acc1[t, 0])
+            evac(False, ds[t][:, cols(1)], acc1[t, 1])
+        pair_up(2)
+        pair_up(3)
+
+        def interleave(dst, src, scalar_cols):
+            dv = dst[:].rearrange("p (c i t) -> p c t i", i=4, t=PACK)
+            sv = src[:].rearrange("p t (c i) -> p c t i", i=4)
+            cut = (HALF - scalar_cols) // 4
+            nc.vector.tensor_copy(dv[:, 0:cut], sv[:, 0:cut])
+            if scalar_cols:
+                nc.scalar.copy(dv[:, cut:], sv[:, cut:])
+
+        h2 = [keep.tile([P, S], F32, name="h2_%d" % t) for t in range(PACK)]
+        dg = [keep.tile([P, S], F32, name="dg%d" % t) for t in range(PACK)]
+        g3 = {}
+
+        def weigh(t):
+            nc.scalar.activation(dg[t][:], ds[t][:], ACT.Copy, scale=g_s[:, t : t + 1])
+
+        def fetch3(on_vector, t, hf):
+            g3[t, hf] = keep.tile([P, HALF], F32, name="g3_%d%d" % (t, hf))
+            fetch(on_vector, g3[t, hf][:], dg[t], entries(l_n3, hf))
+
+        weigh(0)
+        weigh(1)
+        weigh(2)
+        fetch3(False, 0, 0)
+        weigh(3)
+        fetch3(True, 1, 0)
+        fetch3(True, 2, 0)
+        fetch3(False, 3, 0)
+        for t in range(PACK):
+            fetch3(False, t, 1)
+        acc2 = {}
+        for hf in range(2):
+            zb = keep.tile([P, PACK, HALF], BF16, name="zb%d" % hf)
+            for t in range(PACK):
+                nc.vector.scalar_tensor_tensor(zb[:, t, :], g3[t, hf][:], -0.5, dg[t][:, cols(hf)], ALU.mult, ALU.add)
+            zi = keep.tile([P, PACK * HALF], BF16, name="zi%d" % hf, align_bytes=64)
+            z_c = keep.tile([P, HALF], U32, name="z_c%d" % hf, align_bytes=64)
+            z_s = keep.tile([P, HALF], U8, name="z_s%d" % hf, align_bytes=64)
+            interleave(zi, zb, 80 * hf)
+            nc.vector.quantize_mx(out=z_c[:].bitcast(FP8X4), scales=z_s[:], in_=zi[:])
+            for t in range(PACK):
+                acc2[t, hf] = product(t, hf, z_c[:], z_s[:])
+        for t in range(PACK):
+            evac(False, h2[t][:, cols(0)], acc2[t, 0])
+        for t in range(PACK):
+            evac(t > 0, h2[t][:, cols(1)], acc2[t, 1])
+
+        st = [keep.tile([P, S], F32, name="st%d" % t) for t in range(PACK)]
+        res = [keep.tile([P, PACK, HALF], F32, name="res%d" % hf) for hf in range(2)]
+        out_rows = out_0.rearrange("(p t) j -> p t j", t=PACK)
+        g5 = {}
+
+        def fetch5(on_vector, t, hf):
+            g5[t, hf] = keep.tile([P, HALF], F32, name="g5_%d%d" % (t, hf))
+            fetch(on_vector, g5[t, hf][:], st[t], entries(l_n5, hf))
+
+        def finish(t, hf):
+            nc.vector.tensor_tensor(res[hf][:, t, :], st[t][:, cols(hf)], g5[t, hf][:], ALU.subtract)
+            nc.sync.dma_start(out_rows[:, t, cols(hf)], res[hf][:, t, :])
+
+        for t in range(PACK):
+            for hf in range(2):
+                sg = keep.tile([P, HALF], F32, name="sg%d%d" % (t, hf))
+                nc.scalar.activation(sg[:], h2[t][:].indirect(entries(l_n4, hf)), ACT.Sigmoid)
+                nc.vector.tensor_tensor(st[t][:, cols(hf)], h2[t][:, cols(hf)], sg[:], ALU.mult)
+            if t == 0:
+                fetch5(True, 0, 0)
+                fetch5(True, 0, 1)
+            if t == 1:
+                finish(0, 0)
+                finish(0, 1)
+        fetch5(True, 1, 1)
+
+        o_c = keep.tile([P, S], U32, name="o_c", align_bytes=64)
+        o_s = keep.tile([P, S], U8, name="o_s", align_bytes=64)
+        out_words = out_1[0].rearrange("p n t -> p (n t)").bitcast(I32)
+        for hf in range(2):
+            for t in range(1, PACK):
+                if (t, hf) not in g5:
+                    fetch5(False, t, hf)
+                finish(t, hf)
+            oi = keep.tile([P, PACK * HALF], BF16, name="oi%d" % hf, align_bytes=64)
+            interleave(oi, res[hf], 80 * hf)
+            nc.vector.quantize_mx(out=o_c[:, cols(hf)].bitcast(FP8X4), scales=o_s[:, cols(hf)], in_=oi[:])
+            nc.sync.dma_start(out_words[:, cols(hf)], o_c[:, cols(hf)].bitcast(I32))
+        for q in range(4):
+            eng = nc.scalar if q % 2 else nc.sync
+            eng.dma_start(out_2[0, 4 * q : 4 * q + 4, :].bitcast(I32), o_s[32 * q : 32 * q + 4, :].bitcast(I32))

@@ -43,6 +43,9 @@ def tile_picked_ringfolddhopg_none_po_kernel(
         x_sc = keep.tile([P, TABLE], U8, name="x_sc")
         planes = keep.tile([P, 2 * S], U8, name="planes", align_bytes=64)
         nc.vector.memset(planes[:].bitcast(I32), 0)
+        warm = keep.tile([P, 16], F32, name="warm")
+        nc.gpsimd.memset(warm[:, 0:8], 0.0)
+        nc.scalar.activation(warm[:, 8:9], warm[:, 0:1], ACT.Sigmoid)
 
         def load_scales(dst, src):
             rows = src[0].bitcast(I32)

@@ -120,13 +120,15 @@ def tile_picked_ringfolddhopg_none_po_kernel(
             acc1[t, hf] = product(t, hf, x_wg[hf][:], planes[:, S + hf * HALF : S + (hf + 1) * HALF])
 
         ds = [keep.tile([P, S], F32, name="ds%d" % t) for t in range(PACK)]
+        h2 = [keep.tile([P, 2 * S], F32, name="h2_%d" % t) for t in range(PACK)]
+        st = [keep.tile([P, 2 * S], F32, name="st%d" % t) for t in range(PACK)]
 
         def pair_up(t):
-            pa = keep.tile([P, HALF], F32, name="pa%d" % t)
-            pb = keep.tile([P, HALF], F32, name="pb%d" % t)
-            nc.scalar.activation(pb[:], ds[t][:].indirect(l_n2[:]), ACT.Copy, scale=-0.5)
-            fetch(t == 0, pa[:], ds[t], l_n1[:])
-            nc.vector.tensor_tensor(ds[t][:].indirect(l_n2[:]), pa[:], pb[:], ALU.add)
+            pa = h2[t][:, S : S + HALF]
+            pb = h2[t][:, S + HALF : 2 * S]
+            nc.scalar.activation(pb, ds[t][:].indirect(l_n2[:]), ACT.Copy, scale=-0.5)
+            fetch(t == 0, pa, ds[t], l_n1[:])
+            nc.vector.tensor_tensor(ds[t][:].indirect(l_n2[:]), pa, pb, ALU.add)
 
         for t in range(2):
             evac(False, ds[t][:, cols(0)], acc1[t, 0])
@@ -141,13 +143,12 @@ def tile_picked_ringfolddhopg_none_po_kernel(
 
         def interleave(dst, src, scalar_cols):
             dv = dst[:].rearrange("p (c i t) -> p c t i", i=4, t=PACK)
-            sv = src[:].rearrange("p t (c i) -> p c t i", i=4)
+            sv = src.rearrange("p t (c i) -> p c t i", i=4)
             cut = (HALF - scalar_cols) // 4
             nc.vector.tensor_copy(dv[:, 0:cut], sv[:, 0:cut])
             if scalar_cols:
                 nc.scalar.copy(dv[:, cut:], sv[:, cut:])
 
-        h2 = [keep.tile([P, S], F32, name="h2_%d" % t) for t in range(PACK)]
         dg = [keep.tile([P, S], F32, name="dg%d" % t) for t in range(PACK)]
         g3 = {}
 
@@ -155,8 +156,8 @@ def tile_picked_ringfolddhopg_none_po_kernel(
             nc.scalar.activation(dg[t][:], ds[t][:], ACT.Copy, scale=g_s[:, t : t + 1])
 
         def fetch3(on_vector, t, hf):
-            g3[t, hf] = keep.tile([P, HALF], F32, name="g3_%d%d" % (t, hf))
-            fetch(on_vector, g3[t, hf][:], dg[t], entries(l_n3, hf))
+            g3[t, hf] = st[t][:, S + hf * HALF : S + (hf + 1) * HALF]
+            fetch(on_vector, g3[t, hf], dg[t], entries(l_n3, hf))
 
         weigh(0)
         weigh(1)
@@ -172,55 +173,53 @@ def tile_picked_ringfolddhopg_none_po_kernel(
         for hf in range(2):
             zb = keep.tile([P, PACK, HALF], BF16, name="zb%d" % hf)
             for t in range(PACK):
-                nc.vector.scalar_tensor_tensor(zb[:, t, :], g3[t, hf][:], -0.5, dg[t][:, cols(hf)], ALU.mult, ALU.add)
+                nc.vector.scalar_tensor_tensor(zb[:, t, :], g3[t, hf], -0.5, dg[t][:, cols(hf)], ALU.mult, ALU.add)
             zi = keep.tile([P, PACK * HALF], BF16, name="zi%d" % hf, align_bytes=64)
             z_c = keep.tile([P, HALF], U32, name="z_c%d" % hf, align_bytes=64)
             z_s = keep.tile([P, HALF], U8, name="z_s%d" % hf, align_bytes=64)
-            interleave(zi, zb, 80 * hf)
+            interleave(zi, zb[:], 80 * hf)
             nc.vector.quantize_mx(out=z_c[:].bitcast(FP8X4), scales=z_s[:], in_=zi[:])
             for t in range(PACK):
                 acc2[t, hf] = product(t, hf, z_c[:], z_s[:])
         for t in range(PACK):
             evac(False, h2[t][:, cols(0)], acc2[t, 0])
         for t in range(PACK):
-            evac(t > 0, h2[t][:, cols(1)], acc2[t, 1])
+            evac(True, h2[t][:, cols(1)], acc2[t, 1])
 
-        st = [keep.tile([P, S], F32, name="st%d" % t) for t in range(PACK)]
-        res = [keep.tile([P, PACK, HALF], F32, name="res%d" % hf) for hf in range(2)]
+        res = keep.tile([P, PACK, S], F32, name="res")
         out_rows = out_0.rearrange("(p t) j -> p t j", t=PACK)
-        g5 = {}
+        sg = [keep.tile([P, S], F32, name="sg%d" % t) for t in range(PACK)]
+        g5 = [keep.tile([P, S], F32, name="g5_%d" % t) for t in range(PACK)]
 
-        def fetch5(on_vector, t, hf):
-            g5[t, hf] = keep.tile([P, HALF], F32, name="g5_%d%d" % (t, hf))
-            fetch(on_vector, g5[t, hf][:], st[t], entries(l_n5, hf))
+        def gate(t, c, lst):
+            nc.scalar.activation(sg[t][:, c], h2[t][:].indirect(lst), ACT.Sigmoid)
+            nc.vector.tensor_tensor(st[t][:, c], h2[t][:, c], sg[t][:, c], ALU.mult)
 
-        def finish(t, hf):
-            nc.vector.tensor_tensor(res[hf][:, t, :], st[t][:, cols(hf)], g5[t, hf][:], ALU.subtract)
-            nc.sync.dma_start(out_rows[:, t, cols(hf)], res[hf][:, t, :])
+        def finish(t, c):
+            nc.vector.tensor_tensor(res[:, t, c], st[t][:, c], g5[t][:, c], ALU.subtract)
+            nc.sync.dma_start(out_rows[:, t, c], res[:, t, c])
 
-        for t in range(PACK):
-            for hf in range(2):
-                sg = keep.tile([P, HALF], F32, name="sg%d%d" % (t, hf))
-                nc.scalar.activation(sg[:], h2[t][:].indirect(entries(l_n4, hf)), ACT.Sigmoid)
-                nc.vector.tensor_tensor(st[t][:, cols(hf)], h2[t][:, cols(hf)], sg[:], ALU.mult)
-            if t == 0:
-                fetch5(True, 0, 0)
-                fetch5(True, 0, 1)
-            if t == 1:
-                finish(0, 0)
-                finish(0, 1)
-        fetch5(True, 1, 1)
+        whole = slice(0, S)
+        gate(0, cols(0), entries(l_n4, 0))
+        gate(0, cols(1), entries(l_n4, 1))
+        fetch(True, g5[0][:], st[0], l_n5[:])
+        gate(1, whole, l_n4[:])
+        finish(0, whole)
+        gate(2, whole, l_n4[:])
+        gate(3, cols(0), entries(l_n4, 0))
+        gate(3, cols(1), entries(l_n4, 1))
+        fetch(True, g5[1][:, cols(1)], st[1], entries(l_n5, 1))
 
         o_c = keep.tile([P, S], U32, name="o_c", align_bytes=64)
         o_s = keep.tile([P, S], U8, name="o_s", align_bytes=64)
         out_words = out_1[0].rearrange("p n t -> p (n t)").bitcast(I32)
         for hf in range(2):
             for t in range(1, PACK):
-                if (t, hf) not in g5:
-                    fetch5(False, t, hf)
-                finish(t, hf)
+                if (t, hf) != (1, 1):
+                    fetch(False, g5[t][:, cols(hf)], st[t], entries(l_n5, hf))
+                finish(t, cols(hf))
             oi = keep.tile([P, PACK * HALF], BF16, name="oi%d" % hf, align_bytes=64)
-            interleave(oi, res[hf], 80 * hf)
+            interleave(oi, res[:, :, cols(hf)], 80 * hf)
             nc.vector.quantize_mx(out=o_c[:, cols(hf)].bitcast(FP8X4), scales=o_s[:, cols(hf)], in_=oi[:])
             nc.sync.dma_start(out_words[:, cols(hf)], o_c[:, cols(hf)].bitcast(I32))
         for q in range(4):

from contextlib import ExitStack

import concourse.mybir as mybir

F32 = mybir.dt.float32
BF16 = mybir.dt.bfloat16
I32 = mybir.dt.int32
U32 = mybir.dt.uint32
U16 = mybir.dt.uint16
U8 = mybir.dt.uint8
FP8X4 = mybir.dt.float8_e4m3fn_x4
ALU = mybir.AluOpType
ACT = mybir.ActivationFunctionType

P = 128
PACK = 4
TABLE = 2048
S = 512
HALF = 256
FLOPS = 2 * 2 * 512 * 512 * 512


def tile_picked_ringfolddhopg_none_po_kernel(
    tc, x_words, x_scales, d_words, d_scales, gs, offs, k1, n1, n2, n3, n4, n5, out_0, out_1, out_2
):
    nc = tc.nc
    with ExitStack() as ctx:
        keep = ctx.enter_context(tc.tile_pool(name="keep", bufs=1))
        psum = ctx.enter_context(tc.psum_pool(name="psum", bufs=1))

        def load_list(src, name):
            t = keep.tile(list(src.shape), U16, name=name)
            nc.sync.dma_start(t[:], src)
            return t

        def cols(hf):
            return slice(hf * HALF, (hf + 1) * HALF)

        def entries(lst, hf):
            return lst[:, hf * (HALF // 16) : (hf + 1) * (HALF // 16)]

        d_sc = keep.tile([P, TABLE], U8, name="d_sc")
        x_sc = keep.tile([P, TABLE], U8, name="x_sc")
        planes = keep.tile([P, 2 * S], U8, name="planes", align_bytes=64)
        nc.vector.memset(planes[:].bitcast(I32), 0)
        warm = keep.tile([P, 16], F32, name="warm")
        nc.gpsimd.memset(warm[:, 0:8], 0.0)
        nc.scalar.activation(warm[:, 8:9], warm[:, 0:1], ACT.Sigmoid)

        def load_scales(dst, src):
            rows = src[0].bitcast(I32)
            nc.sync.dma_start(dst[:].bitcast(I32), rows.unsqueeze(1).to_broadcast([16, 8, TABLE // 4]))

        l_k1 = load_list(k1, "l_k1")
        load_scales(d_sc, d_scales)
        l_offs = load_list(offs, "l_offs")
        load_scales(x_sc, x_scales)
        l_n1 = load_list(n1, "l_n1")
        l_n2 = load_list(n2, "l_n2")
        d_w = keep.tile([P, TABLE], U32, name="d_w")
        x_w = keep.tile([P, TABLE], U32, name="x_w")
        nc.sync.dma_start(d_w[:].bitcast(I32), d_words[0].rearrange("p n t -> p (n t)").bitcast(I32))
        nc.sync.dma_start(x_w[:].bitcast(I32), x_words[0].rearrange("p n t -> p (n t)").bitcast(I32))

        d_bg = keep.tile([P, S], U8, name="d_bg")
        x_bg = keep.tile([P, S], U8, name="x_bg")
        staged = keep.tile([P, 2 * S], U8, name="staged")
        nc.vector.tensor_copy(d_bg[:], d_sc[:].indirect(l_k1[:]))
        nc.vector.tensor_copy(x_bg[:], x_sc[:].indirect(l_offs[:]))
        nc.vector.tensor_copy(
            staged[:, 0:S].rearrange("p (t m) -> p m t", t=PACK), d_bg[:].rearrange("p (m t) -> p m t", t=PACK)
        )
        nc.vector.tensor_copy(staged[:, S : 2 * S].bitcast(I32), x_bg[:].bitcast(I32))
        for r in range(4):
            nc.scalar.dma_start(planes[r:P:32, :].bitcast(I32), staged[8 * r : P : 32, :].bitcast(I32))

        l_n3 = load_list(n3, "l_n3")
        g_s = keep.tile([P, PACK], F32, name="g_s")
        nc.gpsimd.dma_start(g_s[:], gs.rearrange("(p t) o -> p (t o)", t=PACK))
        l_n4 = load_list(n4, "l_n4")
        l_n5 = load_list(n5, "l_n5")

        d_wg = keep.tile([P, S], U32, name="d_wg")
        d_wd = keep.tile([P, S], U32, name="d_wd", align_bytes=64)
        nc.vector.tensor_copy(d_wg[:], d_w[:].indirect(l_k1[:]))
        nc.vector.tensor_copy(
            d_wd[:].rearrange("p (t m) -> p m t", t=PACK), d_wg[:].rearrange("p (m t) -> p m t", t=PACK)
        )
        x_wg = [keep.tile([P, HALF], U32, name="x_wg%d" % hf, align_bytes=64) for hf in range(2)]

        def product(t, hf, codes, scales):
            acc = psum.tile([P, HALF], F32, name="acc%d%d" % (t, hf), tag="acc%d%d" % (t, hf))
            nc.tensor.matmul_mx(
                out=acc[:],
                lhsT=d_wd[:, t * P : (t + 1) * P].bitcast(FP8X4),
                lhsT_scale=planes[:, t * P : (t + 1) * P],
                rhs=codes.bitcast(FP8X4),
                rhs_scale=scales,
                start=True,
                stop=True,
            )
            return acc

        def evac(on_vector, dst, acc):
            if on_vector:
                nc.vector.tensor_scalar(dst, acc[:], 0.0625, None, ALU.mult)
            else:
                nc.scalar.activation(dst, acc[:], ACT.Copy, scale=0.0625)

        def fetch(on_vector, dst, window, lst):
            if on_vector:
                nc.vector.tensor_copy(dst, window[:].indirect(lst))
            else:
                nc.scalar.activation(dst, window[:].indirect(lst), ACT.Copy)

        acc1 = {}
        for hf in range(2):
            nc.vector.tensor_copy(x_wg[hf][:], x_w[:].indirect(entries(l_offs, hf)))
        for t, hf in ((0, 0), (1, 0), (0, 1), (1, 1), (2, 0), (2, 1), (3, 0), (3, 1)):
            acc1[t, hf] = product(t, hf, x_wg[hf][:], planes[:, S + hf * HALF : S + (hf + 1) * HALF])

        ds = [keep.tile([P, S], F32, name="ds%d" % t) for t in range(PACK)]
        h2 = [keep.tile([P, 2 * S], F32, name="h2_%d" % t) for t in range(PACK)]
        st = [keep.tile([P, 2 * S], F32, name="st%d" % t) for t in range(PACK)]

        def pair_up(t):
            pa = h2[t][:, S : S + HALF]
            pb = h2[t][:, S + HALF : 2 * S]
            nc.scalar.activation(pb, ds[t][:].indirect(l_n2[:]), ACT.Copy, scale=-0.5)
            fetch(t == 0, pa, ds[t], l_n1[:])
            nc.vector.tensor_tensor(ds[t][:].indirect(l_n2[:]), pa, pb, ALU.add)

        for t in range(2):
            evac(False, ds[t][:, cols(0)], acc1[t, 0])
            evac(True, ds[t][:, cols(1)], acc1[t, 1])
        pair_up(0)
        pair_up(1)
        for t in range(2, PACK):
            evac(False, ds[t][:, cols(0)], acc1[t, 0])
            evac(False, ds[t][:, cols(1)], acc1[t, 1])
        pair_up(2)
        pair_up(3)

        def interleave(dst, src, scalar_cols):
            dv = dst[:].rearrange("p (c i t) -> p c t i", i=4, t=PACK)
            sv = src.rearrange("p t (c i) -> p c t i", i=4)
            cut = (HALF - scalar_cols) // 4
            nc.vector.tensor_copy(dv[:, 0:cut], sv[:, 0:cut])
            if scalar_cols:
                nc.scalar.copy(dv[:, cut:], sv[:, cut:])

        dg = [keep.tile([P, S], F32, name="dg%d" % t) for t in range(PACK)]
        g3 = {}

        def weigh(t):
            nc.scalar.activation(dg[t][:], ds[t][:], ACT.Copy, scale=g_s[:, t : t + 1])

        def fetch3(on_vector, t, hf):
            g3[t, hf] = st[t][:, S + hf * HALF : S + (hf + 1) * HALF]
            fetch(on_vector, g3[t, hf], dg[t], entries(l_n3, hf))

        weigh(0)
        weigh(1)
        weigh(2)
        fetch3(False, 0, 0)
        weigh(3)
        fetch3(True, 1, 0)
        fetch3(True, 2, 0)
        fetch3(False, 3, 0)
        for t in range(PACK):
            fetch3(False, t, 1)
        acc2 = {}
        for hf in range(2):
            zb = keep.tile([P, PACK, HALF], BF16, name="zb%d" % hf)
            for t in range(PACK):
                nc.vector.scalar_tensor_tensor(zb[:, t, :], g3[t, hf], -0.5, dg[t][:, cols(hf)], ALU.mult, ALU.add)
            zi = keep.tile([P, PACK * HALF], BF16, name="zi%d" % hf, align_bytes=64)
            z_c = keep.tile([P, HALF], U32, name="z_c%d" % hf, align_bytes=64)
            z_s = keep.tile([P, HALF], U8, name="z_s%d" % hf, align_bytes=64)
            interleave(zi, zb[:], 80 * hf)
            nc.vector.quantize_mx(out=z_c[:].bitcast(FP8X4), scales=z_s[:], in_=zi[:])
            for t in range(PACK):
                acc2[t, hf] = product(t, hf, z_c[:], z_s[:])
        for t in range(PACK):
            evac(False, h2[t][:, cols(0)], acc2[t, 0])
        for t in range(PACK):
            evac(True, h2[t][:, cols(1)], acc2[t, 1])

        res = keep.tile([P, PACK, S], F32, name="res")
        out_rows = out_0.rearrange("(p t) j -> p t j", t=PACK)
        sg = [keep.tile([P, S], F32, name="sg%d" % t) for t in range(PACK)]
        g5 = [keep.tile([P, S], F32, name="g5_%d" % t) for t in range(PACK)]

        def gate(t, c, lst):
            nc.scalar.activation(sg[t][:, c], h2[t][:].indirect(lst), ACT.Sigmoid)
            nc.vector.tensor_tensor(st[t][:, c], h2[t][:, c], sg[t][:, c], ALU.mult)

        def finish(t, c):
            nc.vector.tensor_tensor(res[:, t, c], st[t][:, c], g5[t][:, c], ALU.subtract)
            nc.sync.dma_start(out_rows[:, t, c], res[:, t, c])

        whole = slice(0, S)
        gate(0, cols(0), entries(l_n4, 0))
        gate(0, cols(1), entries(l_n4, 1))
        fetch(True, g5[0][:], st[0], l_n5[:])
        gate(1, whole, l_n4[:])
        finish(0, whole)
        gate(2, whole, l_n4[:])
        gate(3, cols(0), entries(l_n4, 0))
        gate(3, cols(1), entries(l_n4, 1))
        fetch(True, g5[1][:, cols(1)], st[1], entries(l_n5, 1))

        o_c = keep.tile([P, S], U32, name="o_c", align_bytes=64)
        o_s = keep.tile([P, S], U8, name="o_s", align_bytes=64)
        out_words = out_1[0].rearrange("p n t -> p (n t)").bitcast(I32)
        for hf in range(2):
            for t in range(1, PACK):
                if (t, hf) != (1, 1):
                    fetch(False, g5[t][:, cols(hf)], st[t], entries(l_n5, hf))
                finish(t, cols(hf))
            oi = keep.tile([P, PACK * HALF], BF16, name="oi%d" % hf, align_bytes=64)
            interleave(oi, res[:, :, cols(hf)], 80 * hf)
            nc.vector.quantize_mx(out=o_c[:, cols(hf)].bitcast(FP8X4), scales=o_s[:, cols(hf)], in_=oi[:])
            nc.sync.dma_start(out_words[:, cols(hf)], o_c[:, cols(hf)].bitcast(I32))
        for q in range(4):
            eng = nc.scalar if q % 2 else nc.sync
            eng.dma_start(out_2[0, 4 * q : 4 * q + 4, :].bitcast(I32), o_s[32 * q : 32 * q + 4, :].bitcast(I32))
